import numpy as np
import ml_dtypes


def mxq(x, axis, fmt="e4m3"):
    dtype, down = {"e4m3": (ml_dtypes.float8_e4m3fn, 7), "e5m2": (ml_dtypes.float8_e5m2, 14)}[fmt]
    v = np.moveaxis(np.asarray(x, np.float32).astype(ml_dtypes.bfloat16).astype(np.float64), axis, -1)
    blocks = v.reshape(v.shape[:-1] + (-1, 32))
    amax = np.abs(blocks).max(-1, keepdims=True)
    byte = np.maximum(np.where(amax > 0, np.frexp(amax)[1] - 1 + 127, 0) - down, 1)
    scale = np.exp2(byte - 127.0)
    codes = (blocks / scale).astype(np.float32).astype(dtype).astype(np.float64)
    return np.moveaxis((codes * scale).reshape(v.shape), -1, axis)


WIDE = False


def mx_kscale(k):
    if not WIDE:
        return np.ones(k)
    levels = np.array([30, -30])
    if k % 512:
        return np.exp2(np.random.permutation(np.resize(levels, k // 32))).repeat(32)
    a = np.empty((k // 512, 16))
    for p in range(k // 512):
        a[p, :8] = np.random.permutation(np.resize(levels, 8))
        for g in range(8):
            far = levels[np.abs(levels - a[p, g]) >= 10]
            a[p, g + 8] = far[np.random.randint(len(far))]
    return np.exp2(a.ravel()).repeat(32)


def f64(x):
    return np.asarray(x).astype(np.float64)


def striped(idx):
    return np.tile(np.asarray(idx).reshape(-1, 16).T, (8, 1)).astype(np.uint16)


def unstriped(offs):
    return offs[:16].T.reshape(-1).astype(np.int64)


E2M1 = np.array([0.0, 0.5, 1.0, 1.5, 2.0, 3.0, 4.0, 6.0, -0.0, -0.5, -1.0, -1.5, -2.0, -3.0, -4.0, -6.0])


def pack_weight(w, fmt):
    k, n = w.shape
    w = f64(np.asarray(w, np.float32).astype(ml_dtypes.bfloat16)).reshape(k // 32, 32, n)
    amax = np.abs(w).max(1)
    if fmt in ("e4m3", "e5m2"):
        byte = np.frexp(amax)[1] - 1 + 127 - (7 if fmt == "e4m3" else 14)
    else:
        mant, ex = np.frexp(amax / 6.0)
        byte = np.where(mant > 0.5, ex, ex - 1) + 127
    byte = np.clip(np.where(amax > 0, byte, 1), 1, 254)
    scaled = (w * np.exp2(127.0 - byte)[:, None, :]).reshape(k, n).astype(np.float32)
    by_word = np.ascontiguousarray(scaled.reshape(k // 512, 128, 4, n).transpose(0, 1, 3, 2))
    if fmt in ("e4m3", "e5m2"):
        words = by_word.astype(ml_dtypes.float8_e4m3fn if fmt == "e4m3" else ml_dtypes.float8_e5m2).view(np.uint8)
    else:
        c = by_word.astype(ml_dtypes.float4_e2m1fn).view(np.uint8) & 0xF
        words = (c[..., 0::2] | (c[..., 1::2] << 4)).reshape(k // 512, 128, 2 * n)
    return np.ascontiguousarray(words), np.ascontiguousarray(byte.astype(np.uint8).reshape(k // 512, 16, n))


def unpack_weight(words, scales, fmt):
    g, _, n = scales.shape
    words = np.ascontiguousarray(words).reshape(g, 128, n, -1)
    if fmt in ("e4m3", "e5m2"):
        vals = words.view(ml_dtypes.float8_e4m3fn if fmt == "e4m3" else ml_dtypes.float8_e5m2).astype(np.float64)
    else:
        nib = np.empty((g, 128, n, 4), np.uint8)
        nib[..., 0::2] = words & 0xF
        nib[..., 1::2] = words >> 4
        vals = E2M1[nib]
    vals = vals * np.repeat(np.exp2(scales.astype(np.float64) - 127.0), 8, axis=1)[..., None]
    return vals.transpose(0, 1, 3, 2).reshape(g * 512, n)


def sigmoid(v):
    return 1.0 / (1.0 + np.exp(-v))


def sgn(shape):
    return np.random.uniform(0.5, 2.0, shape) * np.where(np.random.standard_normal(shape) < 0, -1.0, 1.0)


K, T, J, R, F, Z, N, O = 512, 1024, 256, 512, 512, 1024, 256, 128


def setup_inputs():
    n = np.random.standard_normal
    idx = np.random.permutation(T)[:J]
    idx2 = np.random.permutation(Z)[:J]
    idx3 = np.random.permutation(J)[:O]
    idx4 = np.random.permutation(J)[:O]
    fk = mx_kscale(K)
    ff = mx_kscale(F)
    fr = mx_kscale(R)
    xtp = pack_weight(n((K, T)) / fk[:, None], "e2m1")
    xop = pack_weight(n((F, Z)) / ff[:, None], "e5m2")
    wp = pack_weight(n((K, R)) * 1 / np.sqrt(K) * fk[:, None] * fr, "e5m2")
    w2p = pack_weight(n((K, R)) * 1 / np.sqrt(K) * fk[:, None] * fr, "e4m3")
    w0p = pack_weight(n((F, R)) * 1 / np.sqrt(F) * ff[:, None] * fr, "e4m3")
    wbp = pack_weight(n((R, N)) * 1 / np.sqrt(R) / fr[:, None], "e4m3")
    wcp = pack_weight(n((R, N)) * 1 / np.sqrt(R) / fr[:, None], "e2m1")
    return {
        "xt_words": xtp[0],
        "xt_scales": xtp[1],
        "xo_words": xop[0],
        "xo_scales": xop[1],
        "w_words": wp[0],
        "w_scales": wp[1],
        "w2_words": w2p[0],
        "w2_scales": w2p[1],
        "w0_words": w0p[0],
        "w0_scales": w0p[1],
        "wb_words": wbp[0],
        "wb_scales": wbp[1],
        "wc_words": wcp[0],
        "wc_scales": wcp[1],
        "so": (np.random.uniform(0.5, 1.6, (N, 1))).astype(np.float32),
        "sp": (sgn((N, 1))).astype(np.float32),
        "bo": (np.random.uniform(-2.0, 2.0, (N, 1))).astype(np.float32),
        "offs": striped(idx),
        "offs2": striped(idx2),
        "offs3": striped(idx3),
        "offs4": striped(idx4),
    }


def reference(xt_words, xt_scales, xo_words, xo_scales, w_words, w_scales, w2_words, w2_scales, w0_words, w0_scales, wb_words, wb_scales, wc_words, wc_scales, so, sp, bo, offs, offs2, offs3, offs4):
    idx = unstriped(offs)
    idx2 = unstriped(offs2)
    idx3 = unstriped(offs3)
    idx4 = unstriped(offs4)
    xtu = unpack_weight(xt_words, xt_scales, "e2m1")
    xou = unpack_weight(xo_words, xo_scales, "e5m2")
    wu = unpack_weight(w_words, w_scales, "e5m2")
    w2u = unpack_weight(w2_words, w2_scales, "e4m3")
    w0u = unpack_weight(w0_words, w0_scales, "e4m3")
    wbu = unpack_weight(wb_words, wb_scales, "e4m3")
    wcu = unpack_weight(wc_words, wc_scales, "e2m1")
    xtidxg = xtu[:, idx]
    a = wu.T @ xtidxg
    xoidx2g = xou[:, idx2]
    b = w2u.T @ xtidxg + w0u.T @ xoidx2g
    hid = np.maximum(a, b)
    hidq = mxq(hid, 0, "e5m2")
    p = wbu.T @ hidq
    q = wcu.T @ hidq
    m0 = np.maximum(p, q)
    y = m0[:, idx3] * f64(so) * sigmoid(m0[:, idx4] * f64(sp) + f64(bo))
    return y

@@ -1,0 +1,201 @@
+from contextlib import ExitStack
+
+import concourse.mybir as mybir
+from concourse.masks import make_identity
+
+K, T, J, R, F, Z, N, O = 512, 1024, 256, 512, 512, 1024, 256, 128
+FLOPS = 2 * (K * R * J + K * R * J + F * R * J + R * N * J + R * N * J)
+
+F32 = mybir.dt.float32
+BF16 = mybir.dt.bfloat16
+I32 = mybir.dt.int32
+U32 = mybir.dt.uint32
+U16 = mybir.dt.uint16
+U8 = mybir.dt.uint8
+E4M3 = mybir.dt.float8_e4m3fn_x4
+E5M2 = mybir.dt.float8_e5m2_x4
+E2M1 = mybir.dt.float4_e2m1fn_x4
+ACT = mybir.ActivationFunctionType
+ALU = mybir.AluOpType
+AXIS = mybir.AxisListType
+
+P = 128
+HALF = 64
+QUAD = 32
+LIVE = 4
+LIST_COLS = P // 16
+
+
+def load_table_scales(queue, window, scales, row):
+    queue.dma_start(window[row:P:QUAD, :].bitcast(I32), scales[0, row:16:LIVE, :].bitcast(I32))
+
+
+def load_weight_scales(queue, staged, cols, scales, quad):
+    rows = scales[0].rearrange("(h q r) c -> q r h c", h=2, q=2)
+    queue.dma_start(staged[QUAD * quad:QUAD * quad + LIVE, :, cols].bitcast(I32), rows[quad].bitcast(I32))
+
+
+def tile_list_outcomegatedmeet_leaned_kernel(
+    tc, xt_words, xt_scales, xo_words, xo_scales, w_words, w_scales, w2_words, w2_scales,
+    w0_words, w0_scales, wb_words, wb_scales, wc_words, wc_scales, so, sp, bo,
+    offs, offs2, offs3, offs4, out,
+):
+    nc = tc.nc
+    with ExitStack() as ctx:
+        sb = ctx.enter_context(tc.tile_pool(name="sb", bufs=1))
+        ps = ctx.enter_context(tc.psum_pool(name="ps", bufs=1))
+
+        def sbuf(name, shape, dtype, tag=None):
+            return sb.tile(shape, dtype, name=name, tag=tag or name, align_bytes=64)
+
+        list_t = sb.tile([P, J // 16], U16, name="list_t")
+        list_z = sb.tile([P, J // 16], U16, name="list_z")
+        list_v = sb.tile([P, O // 16], U16, name="list_v")
+        list_g = sb.tile([P, O // 16], U16, name="list_g")
+
+        xt_w = sbuf("xt_w", [P, T], U16)
+        xt_s = sbuf("xt_s", [P, T], U8)
+        xo_w = sbuf("xo_w", [P, Z], U32)
+        xo_s = sbuf("xo_s", [P, Z], U8)
+        w_w = sbuf("w_w", [P, R], U32)
+        w2_w = sbuf("w2_w", [P, R], U32)
+        w0_w = sbuf("w0_w", [P, R], U32)
+        wb_w = sbuf("wb_w", [P, N], U32)
+        wc_w = sbuf("wc_w", [P, N], U16)
+        w_s = sbuf("w_s", [P, 2, R], U8)
+        w2_s = sbuf("w2_s", [P, 2, R], U8)
+        w0_s = sbuf("w0_s", [P, R], U8)
+        wb_s = sbuf("wb_s", [P, N], U8)
+        wc_s = sbuf("wc_s", [P, N], U8)
+        xo_staged = sbuf("xo_staged", [P, 2, Z], U8)
+        so_t = sbuf("so_t", [P, 2], F32)
+        sp_t = sbuf("sp_t", [P, 2], F32)
+        bo_t = sbuf("bo_t", [P, 2], F32)
+        ident = sbuf("ident", [P, P], F32)
+
+        def clear(engine, tile_ap):
+            engine.memset(tile_ap.bitcast(I32), 0)
+
+        def clear_staged(engine, staged):
+            clear(engine, staged[0:HALF].rearrange("p h c -> p (h c)"))
+
+        def spread(staged):
+            nc.vector.tensor_copy(staged[HALF:P, 0, :].bitcast(I32), staged[0:HALF, 1, :].bitcast(I32))
+
+        clear(nc.vector, xt_s[:])
+        clear_staged(nc.gpsimd, w_s)
+        clear(nc.gpsimd, w0_s[:])
+        clear_staged(nc.vector, w2_s)
+        clear_staged(nc.vector, xo_staged)
+        clear(nc.vector, wc_s[:])
+        clear(nc.vector, wb_s[:])
+
+        def load_words(queue, tile, words):
+            queue.dma_start(tile[:].bitcast(I32), words.bitcast(I32))
+
+        flat = "p n t -> p (n t)"
+        all_r = slice(0, R)
+        nc.sync.dma_start(list_t[:], offs)
+        load_words(nc.scalar, xt_w, xt_words[0])
+        for row in range(LIVE):
+            load_table_scales((nc.sync, nc.scalar)[row % 2], xt_s, xt_scales, row)
+        load_weight_scales(nc.sync, w_s, all_r, w_scales, 0)
+        load_words(nc.scalar, w_w, w_words[0].rearrange(flat))
+        load_weight_scales(nc.sync, w_s, all_r, w_scales, 1)
+        load_words(nc.scalar, w2_w, w2_words[0].rearrange(flat))
+        nc.sync.dma_start(list_z[:], offs2)
+        load_words(nc.scalar, xo_w, xo_words[0].rearrange(flat))
+        for quad in range(2):
+            load_weight_scales(nc.sync, w2_s, all_r, w2_scales, quad)
+        for quad in range(2):
+            load_weight_scales(nc.sync, xo_staged, slice(0, Z), xo_scales, quad)
+        load_words(nc.sync, w0_w, w0_words[0].rearrange(flat))
+        for row in range(LIVE):
+            load_table_scales((nc.sync, nc.gpsimd)[row % 2], w0_s, w0_scales, row)
+        make_identity(nc, ident[:])
+        for row in range(LIVE):
+            load_table_scales(nc.sync, wb_s, wb_scales, row)
+            load_table_scales(nc.gpsimd, wc_s, wc_scales, row)
+        load_words(nc.sync, wb_w, wb_words[0].rearrange(flat))
+        load_words(nc.sync, wc_w, wc_words[0])
+        nc.sync.dma_start(list_g[:], offs4)
+        with nc.allow_non_contiguous_dma(reason="one value a partition for each half of the output features"):
+            for tile, vec in ((sp_t, sp), (bo_t, bo), (so_t, so)):
+                nc.sync.dma_start(tile[:], vec.rearrange("(h p) o -> p (h o)", h=2))
+        nc.sync.dma_start(list_v[:], offs3)
+
+        xt_gw = sbuf("xt_gw", [P, J], U16)
+        xt_gs = sbuf("xt_gs", [P, J], U8)
+        xo_gs = sbuf("xo_gs", [P, J], U8)
+
+        nc.vector.tensor_copy(xt_gs[:], xt_s[:].indirect(list_t[:]))
+        nc.vector.tensor_copy(xt_gw[:], xt_w[:].indirect(list_t[:]))
+        spread(w_s)
+        spread(w2_s)
+        for half in range(2):
+            nc.vector.tensor_copy(xo_s[half * HALF:(half + 1) * HALF, :].bitcast(I32),
+                                  xo_staged[0:HALF, half, :].bitcast(I32))
+        nc.vector.tensor_copy(xo_gs[:], xo_s[:].indirect(list_z[:]))
+        xo_gw = sbuf("xo_gw", [P, J], U32, tag="xo_s")
+        for jt in range(2):
+            nc.vector.tensor_copy(
+                xo_gw[:, jt * P:(jt + 1) * P], xo_w[:].indirect(list_z[:, jt * LIST_COLS:(jt + 1) * LIST_COLS])
+            )
+
+        a_ps = [ps.tile([P, R], F32, name="a_ps%d" % jt, tag="bank%d" % jt) for jt in range(2)]
+        b_ps = [ps.tile([P, R], F32, name="b_ps%d" % jt, tag="bank%d" % (2 + jt)) for jt in range(2)]
+        a_sb = [sbuf("a_sb%d" % jt, [P, R], F32) for jt in range(2)]
+        order = "j (p u e) -> j u p e"
+        for jt in range(2):
+            cols = slice(jt * P, (jt + 1) * P)
+            nc.tensor.matmul_mx(a_ps[jt][:], lhsT=xt_gw[:, cols].bitcast(E2M1), lhsT_scale=xt_gs[:, cols],
+                                rhs=w_w[:].bitcast(E5M2), rhs_scale=w_s[:, 0, :], start=True, stop=True)
+            nc.scalar.activation(a_sb[jt][:].rearrange("j (u p e) -> j u p e", u=2, e=2),
+                                 a_ps[jt][:].rearrange(order, u=2, e=2), ACT.Copy)
+        for jt in range(2):
+            cols = slice(jt * P, (jt + 1) * P)
+            nc.tensor.matmul_mx(b_ps[jt][:], lhsT=xt_gw[:, cols].bitcast(E2M1), lhsT_scale=xt_gs[:, cols],
+                                rhs=w2_w[:].bitcast(E4M3), rhs_scale=w2_s[:, 0, :], start=True, stop=False)
+        for jt in range(2):
+            cols = slice(jt * P, (jt + 1) * P)
+            nc.tensor.matmul_mx(b_ps[jt][:], lhsT=xo_gw[:, cols].bitcast(E5M2), lhsT_scale=xo_gs[:, cols],
+                                rhs=w0_w[:].bitcast(E4M3), rhs_scale=w0_s[:], start=False, stop=True)
+
+        hid = [sbuf("hid%d" % jt, [P, R], BF16) for jt in range(2)]
+        hid_t = [sbuf("hid_t%d" % jt, [P, P, 2], F32) for jt in range(2)]
+        hq_w = [sbuf("hq_w%d" % jt, [P, P], U32) for jt in range(2)]
+        hq_s = [sbuf("hq_s%d" % jt, [P, P], U8) for jt in range(2)]
+        m0 = [sbuf("m0_%d" % h, [P, J], F32) for h in range(2)]
+        for jt in range(2):
+            nc.vector.tensor_tensor(hid[jt][:].rearrange("j (u p e) -> j u p e", u=2, e=2),
+                                    b_ps[jt][:].rearrange(order, u=2, e=2),
+                                    a_sb[jt][:].rearrange("j (u p e) -> j u p e", u=2, e=2), ALU.max)
+        for jt in range(2):
+            turned = ps.tile([P, 2, P], F32, name="turned%d" % jt, tag="bank%d" % (4 + jt))
+            words = hid[jt][:].bitcast(F32)
+            for u in range(2):
+                nc.tensor.transpose(turned[:, u, :], words[:, u * P:(u + 1) * P], ident[:])
+            nc.scalar.copy(hid_t[jt][:], turned[:].rearrange("p u j -> p j u"))
+            nc.vector.quantize_mx(hq_w[jt][:].bitcast(E5M2), hq_s[jt][:],
+                                  hid_t[jt][:].rearrange("p j u -> p (j u)").bitcast(BF16))
+        for jt in range(2):
+            for h in range(2):
+                cols = slice(h * P, (h + 1) * P)
+                pq = ps.tile([P, 2, P], F32, name="pq%d%d" % (jt, h), tag="bank%d" % ((6 + 2 * jt + h) % 8))
+                nc.tensor.matmul_mx(pq[:, 0, :], lhsT=wb_w[:, cols].bitcast(E4M3), lhsT_scale=wb_s[:, cols],
+                                    rhs=hq_w[jt][:].bitcast(E5M2), rhs_scale=hq_s[jt][:], start=True, stop=True)
+                nc.tensor.matmul_mx(pq[:, 1, :], lhsT=wc_w[:, cols].bitcast(E2M1),
+                                    lhsT_scale=wc_s[:, cols],
+                                    rhs=hq_w[jt][:].bitcast(E5M2), rhs_scale=hq_s[jt][:], start=True, stop=True)
+                nc.vector.tensor_reduce(m0[h][:, jt * P:(jt + 1) * P], pq[:].rearrange("p s j -> p j s"),
+                                        AXIS.X, ALU.max)
+
+        for h in range(2):
+            gate = sbuf("gate%d" % h, [P, O], F32)
+            value = sbuf("value%d" % h, [P, O], F32)
+            y = sbuf("y%d" % h, [P, O], F32)
+            nc.scalar.activation(gate[:], m0[h][:].indirect(list_g[:]), ACT.Sigmoid,
+                                 bias=bo_t[:, h:h + 1], scale=sp_t[:, h:h + 1])
+            nc.scalar.activation(value[:], m0[h][:].indirect(list_v[:]), ACT.Copy, scale=so_t[:, h:h + 1])
+            nc.vector.tensor_tensor(y[:], value[:], gate[:], ALU.mult)
+            nc.sync.dma_start(out[h * P:(h + 1) * P, :], y[:])

@@ -35,6 +35,11 @@ def load_weight_scales(queue, staged, cols, scales, quad):
     queue.dma_start(staged[QUAD * quad:QUAD * quad + LIVE, :, cols].bitcast(I32), rows[quad].bitcast(I32))
 
 
+def load_scales_folded(queue, folded, cols, scales):
+    rows = scales[0].rearrange("(q r) c -> r q c", r=LIVE)
+    queue.dma_start(folded[0:LIVE, :, cols].bitcast(I32), rows.bitcast(I32))
+
+
 def tile_list_outcomegatedmeet_leaned_kernel(
     tc, xt_words, xt_scales, xo_words, xo_scales, w_words, w_scales, w2_words, w2_scales,
     w0_words, w0_scales, wb_words, wb_scales, wc_words, wc_scales, so, sp, bo,
@@ -62,11 +67,9 @@ def tile_list_outcomegatedmeet_leaned_kernel(
         w0_w = sbuf("w0_w", [P, R], U32)
         wb_w = sbuf("wb_w", [P, N], U32)
         wc_w = sbuf("wc_w", [P, N], U16)
-        w_s = sbuf("w_s", [P, 2, R], U8)
-        w2_s = sbuf("w2_s", [P, 2, R], U8)
-        w0_s = sbuf("w0_s", [P, R], U8)
-        wb_s = sbuf("wb_s", [P, N], U8)
-        wc_s = sbuf("wc_s", [P, N], U8)
+        w_s = sbuf("w_s", [P, 4, R], U8)
+        wb2_s = sbuf("wb2_s", [P, 4, 2 * R], U8)
+        wo_s = sbuf("wo_s", [P, 4, 2 * N], U8)
         xo_staged = sbuf("xo_staged", [P, 2, Z], U8)
         so_t = sbuf("so_t", [P, 2], F32)
         sp_t = sbuf("sp_t", [P, 2], F32)
@@ -79,16 +82,16 @@ def tile_list_outcomegatedmeet_leaned_kernel(
         def clear_staged(engine, staged):
             clear(engine, staged[0:HALF].rearrange("p h c -> p (h c)"))
 
-        def spread(staged):
-            nc.vector.tensor_copy(staged[HALF:P, 0, :].bitcast(I32), staged[0:HALF, 1, :].bitcast(I32))
+        def spread(folded):
+            for quad in range(1, 4):
+                nc.vector.tensor_copy(folded[QUAD * quad:QUAD * quad + LIVE, 0, :].bitcast(I32),
+                                      folded[0:LIVE, quad, :].bitcast(I32))
 
         clear(nc.vector, xt_s[:])
-        clear_staged(nc.gpsimd, w_s)
-        clear(nc.gpsimd, w0_s[:])
-        clear_staged(nc.vector, w2_s)
+        clear(nc.gpsimd, w_s[:, 0, :])
+        clear(nc.gpsimd, wb2_s[:, 0, :])
         clear_staged(nc.vector, xo_staged)
-        clear(nc.vector, wc_s[:])
-        clear(nc.vector, wb_s[:])
+        clear(nc.gpsimd, wo_s[:, 0, :])
 
         def load_words(queue, tile, words):
             queue.dma_start(tile[:].bitcast(I32), words.bitcast(I32))
@@ -99,25 +102,21 @@ def tile_list_outcomegatedmeet_leaned_kernel(
         load_words(nc.scalar, xt_w, xt_words[0])
         for row in range(LIVE):
             load_table_scales((nc.sync, nc.scalar)[row % 2], xt_s, xt_scales, row)
-        load_weight_scales(nc.sync, w_s, all_r, w_scales, 0)
+        load_scales_folded(nc.sync, w_s, all_r, w_scales)
         load_words(nc.scalar, w_w, w_words[0].rearrange(flat))
-        load_weight_scales(nc.sync, w_s, all_r, w_scales, 1)
-        load_words(nc.scalar, w2_w, w2_words[0].rearrange(flat))
+        load_words(nc.sync, w2_w, w2_words[0].rearrange(flat))
+        load_scales_folded(nc.scalar, wb2_s, slice(0, R), w2_scales)
+        load_scales_folded(nc.sync, wb2_s, slice(R, 2 * R), w0_scales)
         nc.sync.dma_start(list_z[:], offs2)
-        load_words(nc.scalar, xo_w, xo_words[0].rearrange(flat))
         for quad in range(2):
-            load_weight_scales(nc.sync, w2_s, all_r, w2_scales, quad)
-        for quad in range(2):
-            load_weight_scales(nc.sync, xo_staged, slice(0, Z), xo_scales, quad)
-        load_words(nc.sync, w0_w, w0_words[0].rearrange(flat))
-        for row in range(LIVE):
-            load_table_scales((nc.sync, nc.gpsimd)[row % 2], w0_s, w0_scales, row)
+            load_weight_scales(nc.scalar, xo_staged, slice(0, Z), xo_scales, quad)
+        load_words(nc.sync, xo_w, xo_words[0].rearrange(flat))
+        load_words(nc.scalar, w0_w, w0_words[0].rearrange(flat))
         make_identity(nc, ident[:])
-        for row in range(LIVE):
-            load_table_scales(nc.sync, wb_s, wb_scales, row)
-            load_table_scales(nc.gpsimd, wc_s, wc_scales, row)
         load_words(nc.sync, wb_w, wb_words[0].rearrange(flat))
         load_words(nc.sync, wc_w, wc_words[0])
+        load_scales_folded(nc.sync, wo_s, slice(0, N), wb_scales)
+        load_scales_folded(nc.sync, wo_s, slice(N, 2 * N), wc_scales)
         nc.sync.dma_start(list_g[:], offs4)
         with nc.allow_non_contiguous_dma(reason="one value a partition for each half of the output features"):
             for tile, vec in ((sp_t, sp), (bo_t, bo), (so_t, so)):
@@ -131,7 +130,7 @@ def tile_list_outcomegatedmeet_leaned_kernel(
         nc.vector.tensor_copy(xt_gs[:], xt_s[:].indirect(list_t[:]))
         nc.vector.tensor_copy(xt_gw[:], xt_w[:].indirect(list_t[:]))
         spread(w_s)
-        spread(w2_s)
+        spread(wb2_s)
         for half in range(2):
             nc.vector.tensor_copy(xo_s[half * HALF:(half + 1) * HALF, :].bitcast(I32),
                                   xo_staged[0:HALF, half, :].bitcast(I32))
@@ -150,16 +149,16 @@ def tile_list_outcomegatedmeet_leaned_kernel(
             cols = slice(jt * P, (jt + 1) * P)
             nc.tensor.matmul_mx(a_ps[jt][:], lhsT=xt_gw[:, cols].bitcast(E2M1), lhsT_scale=xt_gs[:, cols],
                                 rhs=w_w[:].bitcast(E5M2), rhs_scale=w_s[:, 0, :], start=True, stop=True)
-            nc.scalar.activation(a_sb[jt][:].rearrange("j (u p e) -> j u p e", u=2, e=2),
-                                 a_ps[jt][:].rearrange(order, u=2, e=2), ACT.Copy)
+            nc.scalar.copy(a_sb[jt][:].rearrange("j (u p e) -> j u p e", u=2, e=2),
+                           a_ps[jt][:].rearrange(order, u=2, e=2))
         for jt in range(2):
             cols = slice(jt * P, (jt + 1) * P)
             nc.tensor.matmul_mx(b_ps[jt][:], lhsT=xt_gw[:, cols].bitcast(E2M1), lhsT_scale=xt_gs[:, cols],
-                                rhs=w2_w[:].bitcast(E4M3), rhs_scale=w2_s[:, 0, :], start=True, stop=False)
+                                rhs=w2_w[:].bitcast(E4M3), rhs_scale=wb2_s[:, 0, 0:R], start=True, stop=False)
         for jt in range(2):
             cols = slice(jt * P, (jt + 1) * P)
             nc.tensor.matmul_mx(b_ps[jt][:], lhsT=xo_gw[:, cols].bitcast(E5M2), lhsT_scale=xo_gs[:, cols],
-                                rhs=w0_w[:].bitcast(E4M3), rhs_scale=w0_s[:], start=False, stop=True)
+                                rhs=w0_w[:].bitcast(E4M3), rhs_scale=wb2_s[:, 0, R:2 * R], start=False, stop=True)
 
         hid = [sbuf("hid%d" % jt, [P, R], BF16) for jt in range(2)]
         hid_t = [sbuf("hid_t%d" % jt, [P, P, 2], F32) for jt in range(2)]
@@ -170,6 +169,7 @@ def tile_list_outcomegatedmeet_leaned_kernel(
             nc.vector.tensor_tensor(hid[jt][:].rearrange("j (u p e) -> j u p e", u=2, e=2),
                                     b_ps[jt][:].rearrange(order, u=2, e=2),
                                     a_sb[jt][:].rearrange("j (u p e) -> j u p e", u=2, e=2), ALU.max)
+        spread(wo_s)
         for jt in range(2):
             turned = ps.tile([P, 2, P], F32, name="turned%d" % jt, tag="bank%d" % (4 + jt))
             words = hid[jt][:].bitcast(F32)
@@ -182,10 +182,10 @@ def tile_list_outcomegatedmeet_leaned_kernel(
             for h in range(2):
                 cols = slice(h * P, (h + 1) * P)
                 pq = ps.tile([P, 2, P], F32, name="pq%d%d" % (jt, h), tag="bank%d" % ((6 + 2 * jt + h) % 8))
-                nc.tensor.matmul_mx(pq[:, 0, :], lhsT=wb_w[:, cols].bitcast(E4M3), lhsT_scale=wb_s[:, cols],
+                nc.tensor.matmul_mx(pq[:, 0, :], lhsT=wb_w[:, cols].bitcast(E4M3), lhsT_scale=wo_s[:, 0, cols],
                                     rhs=hq_w[jt][:].bitcast(E5M2), rhs_scale=hq_s[jt][:], start=True, stop=True)
                 nc.tensor.matmul_mx(pq[:, 1, :], lhsT=wc_w[:, cols].bitcast(E2M1),
-                                    lhsT_scale=wc_s[:, cols],
+                                    lhsT_scale=wo_s[:, 0, N + h * P:N + (h + 1) * P],
                                     rhs=hq_w[jt][:].bitcast(E5M2), rhs_scale=hq_s[jt][:], start=True, stop=True)
                 nc.vector.tensor_reduce(m0[h][:, jt * P:(jt + 1) * P], pq[:].rearrange("p s j -> p j s"),
                                         AXIS.X, ALU.max)

@@ -1,7 +1,6 @@
 from contextlib import ExitStack
 
 import concourse.mybir as mybir
-from concourse.masks import make_identity
 
 K, T, J, R, F, Z, N, O = 512, 1024, 256, 512, 512, 1024, 256, 128
 FLOPS = 2 * (K * R * J + K * R * J + F * R * J + R * N * J + R * N * J)
@@ -67,14 +66,13 @@ def tile_list_outcomegatedmeet_leaned_kernel(
         w0_w = sbuf("w0_w", [P, R], U32)
         wb_w = sbuf("wb_w", [P, N], U32)
         wc_w = sbuf("wc_w", [P, N], U16)
-        w_s = sbuf("w_s", [P, 4, R], U8)
-        wb2_s = sbuf("wb2_s", [P, 4, 2 * R], U8)
-        wo_s = sbuf("wo_s", [P, 4, 2 * N], U8)
-        xo_staged = sbuf("xo_staged", [P, 2, Z], U8)
+        ws_folded = sbuf("ws_folded", [P, 4, 3 * R], U8)
+        wb_s = sbuf("wb_s", [P, N], U8)
+        wc_s = sbuf("wc_s", [P, N], U8)
+        xt_staged = sbuf("xt_staged", [P, 2, T], U8)
         so_t = sbuf("so_t", [P, 2], F32)
         sp_t = sbuf("sp_t", [P, 2], F32)
         bo_t = sbuf("bo_t", [P, 2], F32)
-        ident = sbuf("ident", [P, P], F32)
 
         def clear(engine, tile_ap):
             engine.memset(tile_ap.bitcast(I32), 0)
@@ -87,36 +85,36 @@ def tile_list_outcomegatedmeet_leaned_kernel(
                 nc.vector.tensor_copy(folded[QUAD * quad:QUAD * quad + LIVE, 0, :].bitcast(I32),
                                       folded[0:LIVE, quad, :].bitcast(I32))
 
-        clear(nc.vector, xt_s[:])
-        clear(nc.gpsimd, w_s[:, 0, :])
-        clear(nc.gpsimd, wb2_s[:, 0, :])
-        clear_staged(nc.vector, xo_staged)
-        clear(nc.gpsimd, wo_s[:, 0, :])
+        clear(nc.vector, ws_folded[:, 0, 0:2 * R])
+        clear(nc.vector, ws_folded[:, 0, 2 * R:3 * R])
+        clear_staged(nc.gpsimd, xt_staged)
+        clear(nc.vector, xo_s[:])
+        clear(nc.vector, wb_s[:])
+        clear(nc.vector, wc_s[:])
 
         def load_words(queue, tile, words):
             queue.dma_start(tile[:].bitcast(I32), words.bitcast(I32))
 
         flat = "p n t -> p (n t)"
-        all_r = slice(0, R)
         nc.sync.dma_start(list_t[:], offs)
-        load_words(nc.scalar, xt_w, xt_words[0])
-        for row in range(LIVE):
-            load_table_scales((nc.sync, nc.scalar)[row % 2], xt_s, xt_scales, row)
-        load_scales_folded(nc.sync, w_s, all_r, w_scales)
         load_words(nc.scalar, w_w, w_words[0].rearrange(flat))
-        load_words(nc.sync, w2_w, w2_words[0].rearrange(flat))
-        load_scales_folded(nc.scalar, wb2_s, slice(0, R), w2_scales)
-        load_scales_folded(nc.sync, wb2_s, slice(R, 2 * R), w0_scales)
-        nc.sync.dma_start(list_z[:], offs2)
+        for i, scales in enumerate((w_scales, w2_scales, w0_scales)):
+            load_scales_folded((nc.sync, nc.scalar)[i % 2], ws_folded, slice(i * R, (i + 1) * R), scales)
         for quad in range(2):
-            load_weight_scales(nc.scalar, xo_staged, slice(0, Z), xo_scales, quad)
+            load_weight_scales((nc.scalar, nc.sync)[quad], xt_staged, slice(0, T), xt_scales, quad)
+        load_words(nc.scalar, xt_w, xt_words[0])
+        load_words(nc.sync, w2_w, w2_words[0].rearrange(flat))
+        load_words(nc.sync, w0_w, w0_words[0].rearrange(flat))
+        for row in range(LIVE):
+            load_table_scales(nc.sync, xo_s, xo_scales, row)
+        nc.sync.dma_start(list_z[:], offs2)
         load_words(nc.sync, xo_w, xo_words[0].rearrange(flat))
-        load_words(nc.scalar, w0_w, w0_words[0].rearrange(flat))
-        make_identity(nc, ident[:])
         load_words(nc.sync, wb_w, wb_words[0].rearrange(flat))
         load_words(nc.sync, wc_w, wc_words[0])
-        load_scales_folded(nc.sync, wo_s, slice(0, N), wb_scales)
-        load_scales_folded(nc.sync, wo_s, slice(N, 2 * N), wc_scales)
+        for row in range(LIVE):
+            load_table_scales(nc.sync, wb_s, wb_scales, row)
+        for row in range(LIVE):
+            load_table_scales(nc.sync, wc_s, wc_scales, row)
         nc.sync.dma_start(list_g[:], offs4)
         with nc.allow_non_contiguous_dma(reason="one value a partition for each half of the output features"):
             for tile, vec in ((sp_t, sp), (bo_t, bo), (so_t, so)):
@@ -127,13 +125,34 @@ def tile_list_outcomegatedmeet_leaned_kernel(
         xt_gs = sbuf("xt_gs", [P, J], U8)
         xo_gs = sbuf("xo_gs", [P, J], U8)
 
-        nc.vector.tensor_copy(xt_gs[:], xt_s[:].indirect(list_t[:]))
-        nc.vector.tensor_copy(xt_gw[:], xt_w[:].indirect(list_t[:]))
-        spread(w_s)
-        spread(wb2_s)
+        w_d = sbuf("w_d", [P, R], U32)
+        w2_d = sbuf("w2_d", [P, R], U32)
+        w0_d = sbuf("w0_d", [P, R], U32)
+        w_ds = sbuf("w_ds", [P, R], U8)
+        w2_ds = sbuf("w2_ds", [P, R], U8)
+        w0_ds = sbuf("w0_ds", [P, R], U8)
+
+        def deal_words(dealt, words):
+            nc.scalar.copy(dealt[:].rearrange("p (t m) -> p m t", t=4), words[:].rearrange("p (m t) -> p m t", t=4))
+
+        def deal_scales(dealt, i):
+            nc.gpsimd.tensor_copy(dealt[:].rearrange("p (t m) -> p t m", t=4),
+                                  ws_folded[:, 0, i * R:(i + 1) * R].rearrange("p (m t) -> p t m", t=4))
+
+        spread(ws_folded)
+        for i, dealt in enumerate((w_ds, w2_ds, w0_ds)):
+            deal_scales(dealt, i)
+        deal_words(w_d, w_w)
         for half in range(2):
-            nc.vector.tensor_copy(xo_s[half * HALF:(half + 1) * HALF, :].bitcast(I32),
-                                  xo_staged[0:HALF, half, :].bitcast(I32))
+            nc.vector.tensor_copy(xt_s[half * HALF:(half + 1) * HALF, :].bitcast(I32),
+                                  xt_staged[0:HALF, half, :].bitcast(I32))
+        for jt in range(2):
+            cols = slice(jt * P, (jt + 1) * P)
+            entries = list_t[:, jt * LIST_COLS:(jt + 1) * LIST_COLS]
+            nc.vector.tensor_copy(xt_gs[:, cols], xt_s[:].indirect(entries))
+            nc.vector.tensor_copy(xt_gw[:, cols], xt_w[:].indirect(entries))
+        deal_words(w2_d, w2_w)
+        deal_words(w0_d, w0_w)
         nc.vector.tensor_copy(xo_gs[:], xo_s[:].indirect(list_z[:]))
         xo_gw = sbuf("xo_gw", [P, J], U32, tag="xo_s")
         for jt in range(2):
@@ -141,51 +160,46 @@ def tile_list_outcomegatedmeet_leaned_kernel(
                 xo_gw[:, jt * P:(jt + 1) * P], xo_w[:].indirect(list_z[:, jt * LIST_COLS:(jt + 1) * LIST_COLS])
             )
 
-        a_ps = [ps.tile([P, R], F32, name="a_ps%d" % jt, tag="bank%d" % jt) for jt in range(2)]
-        b_ps = [ps.tile([P, R], F32, name="b_ps%d" % jt, tag="bank%d" % (2 + jt)) for jt in range(2)]
-        a_sb = [sbuf("a_sb%d" % jt, [P, R], F32) for jt in range(2)]
-        order = "j (p u e) -> j u p e"
+        a_ps = [ps.tile([P, 4, P], F32, name="a_ps%d" % jt) for jt in range(2)]
+        b_ps = [ps.tile([P, 4, P], F32, name="b_ps%d" % jt) for jt in range(2)]
+        a_sb = [sbuf("a_sb%d" % jt, [P, P, 4], F32) for jt in range(2)]
         for jt in range(2):
             cols = slice(jt * P, (jt + 1) * P)
-            nc.tensor.matmul_mx(a_ps[jt][:], lhsT=xt_gw[:, cols].bitcast(E2M1), lhsT_scale=xt_gs[:, cols],
-                                rhs=w_w[:].bitcast(E5M2), rhs_scale=w_s[:, 0, :], start=True, stop=True)
-            nc.scalar.copy(a_sb[jt][:].rearrange("j (u p e) -> j u p e", u=2, e=2),
-                           a_ps[jt][:].rearrange(order, u=2, e=2))
-        for jt in range(2):
-            cols = slice(jt * P, (jt + 1) * P)
-            nc.tensor.matmul_mx(b_ps[jt][:], lhsT=xt_gw[:, cols].bitcast(E2M1), lhsT_scale=xt_gs[:, cols],
-                                rhs=w2_w[:].bitcast(E4M3), rhs_scale=wb2_s[:, 0, 0:R], start=True, stop=False)
-        for jt in range(2):
-            cols = slice(jt * P, (jt + 1) * P)
-            nc.tensor.matmul_mx(b_ps[jt][:], lhsT=xo_gw[:, cols].bitcast(E5M2), lhsT_scale=xo_gs[:, cols],
-                                rhs=w0_w[:].bitcast(E4M3), rhs_scale=wb2_s[:, 0, R:2 * R], start=False, stop=True)
+            for t in range(4):
+                rows = slice(t * P, (t + 1) * P)
+                nc.tensor.matmul_mx(a_ps[jt][:, t, :], lhsT=w_d[:, rows].bitcast(E5M2), lhsT_scale=w_ds[:, rows],
+                                    rhs=xt_gw[:, cols].bitcast(E2M1), rhs_scale=xt_gs[:, cols], start=True, stop=True)
+            nc.scalar.copy(a_sb[jt][:], a_ps[jt][:].rearrange("p t j -> p j t"))
 
-        hid = [sbuf("hid%d" % jt, [P, R], BF16) for jt in range(2)]
-        hid_t = [sbuf("hid_t%d" % jt, [P, P, 2], F32) for jt in range(2)]
+        def b_passes(jt, weight, weight_s, moving, moving_s, first):
+            cols = slice(jt * P, (jt + 1) * P)
+            for t in range(4):
+                rows = slice(t * P, (t + 1) * P)
+                nc.tensor.matmul_mx(b_ps[jt][:, t, :], lhsT=weight[:, rows].bitcast(E4M3), lhsT_scale=weight_s[:, rows],
+                                    rhs=moving[:, cols], rhs_scale=moving_s[:, cols],
+                                    start=(first and t == 0), stop=(not first and t == 3))
+
+        tokens = (w2_d, w2_ds, xt_gw[:].bitcast(E2M1), xt_gs)
+        notes = (w0_d, w0_ds, xo_gw[:].bitcast(E5M2), xo_gs)
+        for jt, (early, late) in enumerate(((tokens, notes), (notes, tokens))):
+            b_passes(jt, *early, True)
+            b_passes(jt, *late, False)
+
+        hid = [sbuf("hid%d" % jt, [P, P, 4], BF16) for jt in range(2)]
         hq_w = [sbuf("hq_w%d" % jt, [P, P], U32) for jt in range(2)]
         hq_s = [sbuf("hq_s%d" % jt, [P, P], U8) for jt in range(2)]
         m0 = [sbuf("m0_%d" % h, [P, J], F32) for h in range(2)]
         for jt in range(2):
-            nc.vector.tensor_tensor(hid[jt][:].rearrange("j (u p e) -> j u p e", u=2, e=2),
-                                    b_ps[jt][:].rearrange(order, u=2, e=2),
-                                    a_sb[jt][:].rearrange("j (u p e) -> j u p e", u=2, e=2), ALU.max)
-        spread(wo_s)
+            nc.vector.tensor_tensor(hid[jt][:], b_ps[jt][:].rearrange("p t j -> p j t"), a_sb[jt][:], ALU.max)
         for jt in range(2):
-            turned = ps.tile([P, 2, P], F32, name="turned%d" % jt, tag="bank%d" % (4 + jt))
-            words = hid[jt][:].bitcast(F32)
-            for u in range(2):
-                nc.tensor.transpose(turned[:, u, :], words[:, u * P:(u + 1) * P], ident[:])
-            nc.scalar.copy(hid_t[jt][:], turned[:].rearrange("p u j -> p j u"))
-            nc.vector.quantize_mx(hq_w[jt][:].bitcast(E5M2), hq_s[jt][:],
-                                  hid_t[jt][:].rearrange("p j u -> p (j u)").bitcast(BF16))
-        for jt in range(2):
-            for h in range(2):
-                cols = slice(h * P, (h + 1) * P)
-                pq = ps.tile([P, 2, P], F32, name="pq%d%d" % (jt, h), tag="bank%d" % ((6 + 2 * jt + h) % 8))
-                nc.tensor.matmul_mx(pq[:, 0, :], lhsT=wb_w[:, cols].bitcast(E4M3), lhsT_scale=wo_s[:, 0, cols],
+            nc.vector.quantize_mx(hq_w[jt][:].bitcast(E5M2), hq_s[jt][:], hid[jt][:].rearrange("p j t -> p (j t)"))
+        for h in range(2):
+            cols = slice(h * P, (h + 1) * P)
+            for jt in range(2):
+                pq = ps.tile([P, 2, P], F32, name="pq%d%d" % (jt, h))
+                nc.tensor.matmul_mx(pq[:, 0, :], lhsT=wb_w[:, cols].bitcast(E4M3), lhsT_scale=wb_s[:, cols],
                                     rhs=hq_w[jt][:].bitcast(E5M2), rhs_scale=hq_s[jt][:], start=True, stop=True)
-                nc.tensor.matmul_mx(pq[:, 1, :], lhsT=wc_w[:, cols].bitcast(E2M1),
-                                    lhsT_scale=wo_s[:, 0, N + h * P:N + (h + 1) * P],
+                nc.tensor.matmul_mx(pq[:, 1, :], lhsT=wc_w[:, cols].bitcast(E2M1), lhsT_scale=wc_s[:, cols],
                                     rhs=hq_w[jt][:].bitcast(E5M2), rhs_scale=hq_s[jt][:], start=True, stop=True)
                 nc.vector.tensor_reduce(m0[h][:, jt * P:(jt + 1) * P], pq[:].rearrange("p s j -> p j s"),
                                         AXIS.X, ALU.max)

@@ -19,24 +19,32 @@ ALU = mybir.AluOpType
 AXIS = mybir.AxisListType
 
 P = 128
-HALF = 64
+PACK = 4
 QUAD = 32
+QUADS = P // QUAD
 LIVE = 4
-LIST_COLS = P // 16
+HALF = P // 2
+STRIPE = 16
+SLOT_TILES = J // P
+FEATURE_TILES = N // P
 
 
-def load_table_scales(queue, window, scales, row):
-    queue.dma_start(window[row:P:QUAD, :].bitcast(I32), scales[0, row:16:LIVE, :].bitcast(I32))
+def load_scale_rows(queue, plane, scales, i):
+    queue.dma_start(plane[i:P:QUAD, :].bitcast(I32), scales[0, i:QUADS * LIVE:LIVE, :].bitcast(I32))
 
 
-def load_weight_scales(queue, staged, cols, scales, quad):
+def load_scales_halved(queue, staged, scales, quad):
     rows = scales[0].rearrange("(h q r) c -> q r h c", h=2, q=2)
-    queue.dma_start(staged[QUAD * quad:QUAD * quad + LIVE, :, cols].bitcast(I32), rows[quad].bitcast(I32))
+    queue.dma_start(staged[QUAD * quad:QUAD * quad + LIVE, :, :].bitcast(I32), rows[quad].bitcast(I32))
 
 
 def load_scales_folded(queue, folded, cols, scales):
     rows = scales[0].rearrange("(q r) c -> r q c", r=LIVE)
     queue.dma_start(folded[0:LIVE, :, cols].bitcast(I32), rows.bitcast(I32))
+
+
+def load_words(queue, tile, words):
+    queue.dma_start(tile[:].bitcast(I32), words.bitcast(I32))
 
 
 def tile_list_outcomegatedmeet_leaned_kernel(
@@ -52,10 +60,10 @@ def tile_list_outcomegatedmeet_leaned_kernel(
         def sbuf(name, shape, dtype, tag=None):
             return sb.tile(shape, dtype, name=name, tag=tag or name, align_bytes=64)
 
-        list_t = sb.tile([P, J // 16], U16, name="list_t")
-        list_z = sb.tile([P, J // 16], U16, name="list_z")
-        list_v = sb.tile([P, O // 16], U16, name="list_v")
-        list_g = sb.tile([P, O // 16], U16, name="list_g")
+        token_list = sb.tile([P, J // STRIPE], U16, name="token_list")
+        note_list = sb.tile([P, J // STRIPE], U16, name="note_list")
+        value_list = sb.tile([P, O // STRIPE], U16, name="value_list")
+        gate_list = sb.tile([P, O // STRIPE], U16, name="gate_list")
 
         xt_w = sbuf("xt_w", [P, T], U16)
         xt_s = sbuf("xt_s", [P, T], U8)
@@ -66,150 +74,142 @@ def tile_list_outcomegatedmeet_leaned_kernel(
         w0_w = sbuf("w0_w", [P, R], U32)
         wb_w = sbuf("wb_w", [P, N], U32)
         wc_w = sbuf("wc_w", [P, N], U16)
-        ws_folded = sbuf("ws_folded", [P, 4, 3 * R], U8)
+        ws_folded = sbuf("ws_folded", [P, QUADS, 3 * R], U8)
         wb_s = sbuf("wb_s", [P, N], U8)
         wc_s = sbuf("wc_s", [P, N], U8)
         xt_staged = sbuf("xt_staged", [P, 2, T], U8)
-        so_t = sbuf("so_t", [P, 2], F32)
-        sp_t = sbuf("sp_t", [P, 2], F32)
-        bo_t = sbuf("bo_t", [P, 2], F32)
+        so_t = sbuf("so_t", [P, FEATURE_TILES], F32)
+        sp_t = sbuf("sp_t", [P, FEATURE_TILES], F32)
+        bo_t = sbuf("bo_t", [P, FEATURE_TILES], F32)
 
-        def clear(engine, tile_ap):
-            engine.memset(tile_ap.bitcast(I32), 0)
+        def clear(engine, scale_bytes):
+            engine.memset(scale_bytes.bitcast(I32), 0)
 
-        def clear_staged(engine, staged):
-            clear(engine, staged[0:HALF].rearrange("p h c -> p (h c)"))
-
-        def spread(folded):
-            for quad in range(1, 4):
-                nc.vector.tensor_copy(folded[QUAD * quad:QUAD * quad + LIVE, 0, :].bitcast(I32),
-                                      folded[0:LIVE, quad, :].bitcast(I32))
-
-        clear(nc.vector, ws_folded[:, 0, 0:2 * R])
-        clear(nc.vector, ws_folded[:, 0, 2 * R:3 * R])
-        clear_staged(nc.gpsimd, xt_staged)
+        clear(nc.gpsimd, ws_folded[:, 0, 0:2 * R])
+        clear(nc.gpsimd, ws_folded[:, 0, 2 * R:3 * R])
+        clear(nc.vector, xt_staged[0:HALF].rearrange("p h c -> p (h c)"))
         clear(nc.vector, xo_s[:])
-        clear(nc.vector, wb_s[:])
         clear(nc.vector, wc_s[:])
+        clear(nc.vector, wb_s[:])
 
-        def load_words(queue, tile, words):
-            queue.dma_start(tile[:].bitcast(I32), words.bitcast(I32))
+        def load_feature_values(queue, tile, values):
+            with nc.allow_non_contiguous_dma(reason="one value a partition for each tile of output features"):
+                queue.dma_start(tile[:], values.rearrange("(h p) o -> p (h o)", h=FEATURE_TILES))
 
         flat = "p n t -> p (n t)"
-        nc.sync.dma_start(list_t[:], offs)
+        nc.sync.dma_start(token_list[:], offs)
         load_words(nc.scalar, w_w, w_words[0].rearrange(flat))
         for i, scales in enumerate((w_scales, w2_scales, w0_scales)):
             load_scales_folded((nc.sync, nc.scalar)[i % 2], ws_folded, slice(i * R, (i + 1) * R), scales)
-        for quad in range(2):
-            load_weight_scales((nc.scalar, nc.sync)[quad], xt_staged, slice(0, T), xt_scales, quad)
+        for quad, queue in enumerate((nc.scalar, nc.sync)):
+            load_scales_halved(queue, xt_staged, xt_scales, quad)
         load_words(nc.scalar, xt_w, xt_words[0])
         load_words(nc.sync, w2_w, w2_words[0].rearrange(flat))
         load_words(nc.sync, w0_w, w0_words[0].rearrange(flat))
-        for row in range(LIVE):
-            load_table_scales(nc.sync, xo_s, xo_scales, row)
-        nc.sync.dma_start(list_z[:], offs2)
+        for i in range(LIVE):
+            load_scale_rows(nc.sync, xo_s, xo_scales, i)
+        nc.sync.dma_start(note_list[:], offs2)
         load_words(nc.sync, xo_w, xo_words[0].rearrange(flat))
+        nc.sync.dma_start(gate_list[:], offs4)
+        load_feature_values(nc.gpsimd, sp_t, sp)
+        load_feature_values(nc.gpsimd, bo_t, bo)
         load_words(nc.sync, wb_w, wb_words[0].rearrange(flat))
         load_words(nc.sync, wc_w, wc_words[0])
-        for row in range(LIVE):
-            load_table_scales(nc.sync, wb_s, wb_scales, row)
-        for row in range(LIVE):
-            load_table_scales(nc.sync, wc_s, wc_scales, row)
-        nc.sync.dma_start(list_g[:], offs4)
-        with nc.allow_non_contiguous_dma(reason="one value a partition for each half of the output features"):
-            for tile, vec in ((sp_t, sp), (bo_t, bo), (so_t, so)):
-                nc.sync.dma_start(tile[:], vec.rearrange("(h p) o -> p (h o)", h=2))
-        nc.sync.dma_start(list_v[:], offs3)
+        for i in range(LIVE):
+            load_scale_rows(nc.sync, wc_s, wc_scales, i)
+        for i in range(LIVE):
+            load_scale_rows(nc.sync, wb_s, wb_scales, i)
+        load_feature_values(nc.sync, so_t, so)
+        nc.sync.dma_start(value_list[:], offs3)
 
         xt_gw = sbuf("xt_gw", [P, J], U16)
         xt_gs = sbuf("xt_gs", [P, J], U8)
         xo_gs = sbuf("xo_gs", [P, J], U8)
-
-        w_d = sbuf("w_d", [P, R], U32)
-        w2_d = sbuf("w2_d", [P, R], U32)
-        w0_d = sbuf("w0_d", [P, R], U32)
+        w_dw = sbuf("w_dw", [P, R], U32)
+        w2_dw = sbuf("w2_dw", [P, R], U32)
+        w0_dw = sbuf("w0_dw", [P, R], U32)
         w_ds = sbuf("w_ds", [P, R], U8)
         w2_ds = sbuf("w2_ds", [P, R], U8)
         w0_ds = sbuf("w0_ds", [P, R], U8)
 
         def deal_words(dealt, words):
-            nc.scalar.copy(dealt[:].rearrange("p (t m) -> p m t", t=4), words[:].rearrange("p (m t) -> p m t", t=4))
+            nc.scalar.copy(dealt[:].rearrange("p (t m) -> p m t", t=PACK),
+                           words[:].rearrange("p (m t) -> p m t", t=PACK))
 
-        def deal_scales(dealt, i):
-            nc.gpsimd.tensor_copy(dealt[:].rearrange("p (t m) -> p t m", t=4),
-                                  ws_folded[:, 0, i * R:(i + 1) * R].rearrange("p (m t) -> p t m", t=4))
+        def tile_cols(i):
+            return slice(i * P, (i + 1) * P)
 
-        spread(ws_folded)
+        def tile_entries(offsets, jt):
+            return offsets[:, jt * P // STRIPE:(jt + 1) * P // STRIPE]
+
+        for quad in range(1, QUADS):
+            nc.vector.tensor_copy(ws_folded[QUAD * quad:QUAD * quad + LIVE, 0, :].bitcast(I32),
+                                  ws_folded[0:LIVE, quad, :].bitcast(I32))
         for i, dealt in enumerate((w_ds, w2_ds, w0_ds)):
-            deal_scales(dealt, i)
-        deal_words(w_d, w_w)
+            nc.gpsimd.tensor_copy(dealt[:].rearrange("p (t m) -> p t m", t=PACK),
+                                  ws_folded[:, 0, i * R:(i + 1) * R].rearrange("p (m t) -> p t m", t=PACK))
+        deal_words(w_dw, w_w)
         for half in range(2):
             nc.vector.tensor_copy(xt_s[half * HALF:(half + 1) * HALF, :].bitcast(I32),
                                   xt_staged[0:HALF, half, :].bitcast(I32))
-        for jt in range(2):
-            cols = slice(jt * P, (jt + 1) * P)
-            entries = list_t[:, jt * LIST_COLS:(jt + 1) * LIST_COLS]
-            nc.vector.tensor_copy(xt_gs[:, cols], xt_s[:].indirect(entries))
-            nc.vector.tensor_copy(xt_gw[:, cols], xt_w[:].indirect(entries))
-        deal_words(w2_d, w2_w)
-        deal_words(w0_d, w0_w)
-        nc.vector.tensor_copy(xo_gs[:], xo_s[:].indirect(list_z[:]))
+        for jt in range(SLOT_TILES):
+            nc.vector.tensor_copy(xt_gs[:, tile_cols(jt)], xt_s[:].indirect(tile_entries(token_list, jt)))
+            nc.vector.tensor_copy(xt_gw[:, tile_cols(jt)], xt_w[:].indirect(tile_entries(token_list, jt)))
+        deal_words(w2_dw, w2_w)
+        deal_words(w0_dw, w0_w)
+        nc.vector.tensor_copy(xo_gs[:], xo_s[:].indirect(note_list[:]))
         xo_gw = sbuf("xo_gw", [P, J], U32, tag="xo_s")
-        for jt in range(2):
-            nc.vector.tensor_copy(
-                xo_gw[:, jt * P:(jt + 1) * P], xo_w[:].indirect(list_z[:, jt * LIST_COLS:(jt + 1) * LIST_COLS])
-            )
+        for jt in range(SLOT_TILES):
+            nc.vector.tensor_copy(xo_gw[:, tile_cols(jt)], xo_w[:].indirect(tile_entries(note_list, jt)))
 
-        a_ps = [ps.tile([P, 4, P], F32, name="a_ps%d" % jt) for jt in range(2)]
-        b_ps = [ps.tile([P, 4, P], F32, name="b_ps%d" % jt) for jt in range(2)]
-        a_sb = [sbuf("a_sb%d" % jt, [P, P, 4], F32) for jt in range(2)]
-        for jt in range(2):
-            cols = slice(jt * P, (jt + 1) * P)
-            for t in range(4):
-                rows = slice(t * P, (t + 1) * P)
-                nc.tensor.matmul_mx(a_ps[jt][:, t, :], lhsT=w_d[:, rows].bitcast(E5M2), lhsT_scale=w_ds[:, rows],
-                                    rhs=xt_gw[:, cols].bitcast(E2M1), rhs_scale=xt_gs[:, cols], start=True, stop=True)
+        a_ps = [ps.tile([P, PACK, P], F32, name="a_ps%d" % jt) for jt in range(SLOT_TILES)]
+        b_ps = [ps.tile([P, PACK, P], F32, name="b_ps%d" % jt) for jt in range(SLOT_TILES)]
+        a_sb = [sbuf("a_sb%d" % jt, [P, P, PACK], F32) for jt in range(SLOT_TILES)]
+        for jt in range(SLOT_TILES):
+            for t in range(PACK):
+                nc.tensor.matmul_mx(a_ps[jt][:, t, :],
+                                    lhsT=w_dw[:, tile_cols(t)].bitcast(E5M2), lhsT_scale=w_ds[:, tile_cols(t)],
+                                    rhs=xt_gw[:, tile_cols(jt)].bitcast(E2M1), rhs_scale=xt_gs[:, tile_cols(jt)],
+                                    start=True, stop=True)
             nc.scalar.copy(a_sb[jt][:], a_ps[jt][:].rearrange("p t j -> p j t"))
 
-        def b_passes(jt, weight, weight_s, moving, moving_s, first):
-            cols = slice(jt * P, (jt + 1) * P)
-            for t in range(4):
-                rows = slice(t * P, (t + 1) * P)
-                nc.tensor.matmul_mx(b_ps[jt][:, t, :], lhsT=weight[:, rows].bitcast(E4M3), lhsT_scale=weight_s[:, rows],
-                                    rhs=moving[:, cols], rhs_scale=moving_s[:, cols],
-                                    start=(first and t == 0), stop=(not first and t == 3))
+        tokens = (w2_dw, w2_ds, xt_gw[:].bitcast(E2M1), xt_gs)
+        notes = (w0_dw, w0_ds, xo_gw[:].bitcast(E5M2), xo_gs)
+        for term, (weight_w, weight_s, moving_w, moving_s) in enumerate((tokens, notes)):
+            for jt in range(SLOT_TILES):
+                for t in range(PACK):
+                    nc.tensor.matmul_mx(b_ps[jt][:, t, :],
+                                        lhsT=weight_w[:, tile_cols(t)].bitcast(E4M3),
+                                        lhsT_scale=weight_s[:, tile_cols(t)],
+                                        rhs=moving_w[:, tile_cols(jt)], rhs_scale=moving_s[:, tile_cols(jt)],
+                                        start=(term == 0 and t == 0), stop=(term == 1 and t == PACK - 1))
 
-        tokens = (w2_d, w2_ds, xt_gw[:].bitcast(E2M1), xt_gs)
-        notes = (w0_d, w0_ds, xo_gw[:].bitcast(E5M2), xo_gs)
-        for jt, (early, late) in enumerate(((tokens, notes), (notes, tokens))):
-            b_passes(jt, *early, True)
-            b_passes(jt, *late, False)
-
-        hid = [sbuf("hid%d" % jt, [P, P, 4], BF16) for jt in range(2)]
-        hq_w = [sbuf("hq_w%d" % jt, [P, P], U32) for jt in range(2)]
-        hq_s = [sbuf("hq_s%d" % jt, [P, P], U8) for jt in range(2)]
-        m0 = [sbuf("m0_%d" % h, [P, J], F32) for h in range(2)]
-        for jt in range(2):
+        hid = [sbuf("hid%d" % jt, [P, P, PACK], BF16) for jt in range(SLOT_TILES)]
+        hid_w = [sbuf("hid_w%d" % jt, [P, P], U32) for jt in range(SLOT_TILES)]
+        hid_s = [sbuf("hid_s%d" % jt, [P, P], U8) for jt in range(SLOT_TILES)]
+        m0 = [sbuf("m0_%d" % h, [P, J], F32) for h in range(FEATURE_TILES)]
+        for jt in range(SLOT_TILES):
             nc.vector.tensor_tensor(hid[jt][:], b_ps[jt][:].rearrange("p t j -> p j t"), a_sb[jt][:], ALU.max)
-        for jt in range(2):
-            nc.vector.quantize_mx(hq_w[jt][:].bitcast(E5M2), hq_s[jt][:], hid[jt][:].rearrange("p j t -> p (j t)"))
-        for h in range(2):
-            cols = slice(h * P, (h + 1) * P)
-            for jt in range(2):
-                pq = ps.tile([P, 2, P], F32, name="pq%d%d" % (jt, h))
-                nc.tensor.matmul_mx(pq[:, 0, :], lhsT=wb_w[:, cols].bitcast(E4M3), lhsT_scale=wb_s[:, cols],
-                                    rhs=hq_w[jt][:].bitcast(E5M2), rhs_scale=hq_s[jt][:], start=True, stop=True)
-                nc.tensor.matmul_mx(pq[:, 1, :], lhsT=wc_w[:, cols].bitcast(E2M1), lhsT_scale=wc_s[:, cols],
-                                    rhs=hq_w[jt][:].bitcast(E5M2), rhs_scale=hq_s[jt][:], start=True, stop=True)
-                nc.vector.tensor_reduce(m0[h][:, jt * P:(jt + 1) * P], pq[:].rearrange("p s j -> p j s"),
-                                        AXIS.X, ALU.max)
+        for jt in range(SLOT_TILES):
+            nc.vector.quantize_mx(hid_w[jt][:].bitcast(E5M2), hid_s[jt][:], hid[jt][:].rearrange("p j t -> p (j t)"))
 
-        for h in range(2):
+        for h in range(FEATURE_TILES):
+            for jt in range(SLOT_TILES):
+                pq = ps.tile([P, 2, P], F32, name="pq%d%d" % (jt, h))
+                nc.tensor.matmul_mx(pq[:, 0, :],
+                                    lhsT=wb_w[:, tile_cols(h)].bitcast(E4M3), lhsT_scale=wb_s[:, tile_cols(h)],
+                                    rhs=hid_w[jt][:].bitcast(E5M2), rhs_scale=hid_s[jt][:], start=True, stop=True)
+                nc.tensor.matmul_mx(pq[:, 1, :],
+                                    lhsT=wc_w[:, tile_cols(h)].bitcast(E2M1), lhsT_scale=wc_s[:, tile_cols(h)],
+                                    rhs=hid_w[jt][:].bitcast(E5M2), rhs_scale=hid_s[jt][:], start=True, stop=True)
+                nc.vector.tensor_reduce(m0[h][:, tile_cols(jt)], pq[:].rearrange("p s j -> p j s"), AXIS.X, ALU.max)
+
+        for h in range(FEATURE_TILES):
             gate = sbuf("gate%d" % h, [P, O], F32)
             value = sbuf("value%d" % h, [P, O], F32)
             y = sbuf("y%d" % h, [P, O], F32)
-            nc.scalar.activation(gate[:], m0[h][:].indirect(list_g[:]), ACT.Sigmoid,
+            nc.scalar.activation(gate[:], m0[h][:].indirect(gate_list[:]), ACT.Sigmoid,
                                  bias=bo_t[:, h:h + 1], scale=sp_t[:, h:h + 1])
-            nc.scalar.activation(value[:], m0[h][:].indirect(list_v[:]), ACT.Copy, scale=so_t[:, h:h + 1])
+            nc.scalar.activation(value[:], m0[h][:].indirect(value_list[:]), ACT.Copy, scale=so_t[:, h:h + 1])
             nc.vector.tensor_tensor(y[:], value[:], gate[:], ALU.mult)
-            nc.sync.dma_start(out[h * P:(h + 1) * P, :], y[:])
+            nc.sync.dma_start(out[tile_cols(h), :], y[:])

from contextlib import ExitStack

import concourse.mybir as mybir

K, T, J, R, F, Z, N, O = 512, 1024, 256, 512, 512, 1024, 256, 128
FLOPS = 2 * (K * R * J + K * R * J + F * R * J + R * N * J + R * N * J)

F32 = mybir.dt.float32
BF16 = mybir.dt.bfloat16
I32 = mybir.dt.int32
U32 = mybir.dt.uint32
U16 = mybir.dt.uint16
U8 = mybir.dt.uint8
E4M3 = mybir.dt.float8_e4m3fn_x4
E5M2 = mybir.dt.float8_e5m2_x4
E2M1 = mybir.dt.float4_e2m1fn_x4
ACT = mybir.ActivationFunctionType
ALU = mybir.AluOpType
AXIS = mybir.AxisListType

P = 128
PACK = 4
QUAD = 32
QUADS = P // QUAD
LIVE = 4
HALF = P // 2
STRIPE = 16
SLOT_TILES = J // P
FEATURE_TILES = N // P


def load_scale_rows(queue, plane, scales, i):
    queue.dma_start(plane[i:P:QUAD, :].bitcast(I32), scales[0, i:QUADS * LIVE:LIVE, :].bitcast(I32))


def load_scales_halved(queue, staged, scales, quad):
    rows = scales[0].rearrange("(h q r) c -> q r h c", h=2, q=2)
    queue.dma_start(staged[QUAD * quad:QUAD * quad + LIVE, :, :].bitcast(I32), rows[quad].bitcast(I32))


def load_scales_folded(queue, folded, cols, scales):
    rows = scales[0].rearrange("(q r) c -> r q c", r=LIVE)
    queue.dma_start(folded[0:LIVE, :, cols].bitcast(I32), rows.bitcast(I32))


def load_words(queue, tile, words):
    queue.dma_start(tile[:].bitcast(I32), words.bitcast(I32))


def tile_list_outcomegatedmeet_leaned_kernel(
    tc, xt_words, xt_scales, xo_words, xo_scales, w_words, w_scales, w2_words, w2_scales,
    w0_words, w0_scales, wb_words, wb_scales, wc_words, wc_scales, so, sp, bo,
    offs, offs2, offs3, offs4, out,
):
    nc = tc.nc
    with ExitStack() as ctx:
        sb = ctx.enter_context(tc.tile_pool(name="sb", bufs=1))
        ps = ctx.enter_context(tc.psum_pool(name="ps", bufs=1))

        def sbuf(name, shape, dtype, tag=None):
            return sb.tile(shape, dtype, name=name, tag=tag or name, align_bytes=64)

        token_list = sb.tile([P, J // STRIPE], U16, name="token_list")
        note_list = sb.tile([P, J // STRIPE], U16, name="note_list")
        value_list = sb.tile([P, O // STRIPE], U16, name="value_list")
        gate_list = sb.tile([P, O // STRIPE], U16, name="gate_list")

        xt_w = sbuf("xt_w", [P, T], U16)
        xt_s = sbuf("xt_s", [P, T], U8)
        xo_w = sbuf("xo_w", [P, Z], U32)
        xo_s = sbuf("xo_s", [P, Z], U8)
        w_w = sbuf("w_w", [P, R], U32)
        w2_w = sbuf("w2_w", [P, R], U32)
        w0_w = sbuf("w0_w", [P, R], U32)
        wb_w = sbuf("wb_w", [P, N], U32)
        wc_w = sbuf("wc_w", [P, N], U16)
        ws_folded = sbuf("ws_folded", [P, QUADS, 3 * R], U8)
        wb_s = sbuf("wb_s", [P, N], U8)
        wc_s = sbuf("wc_s", [P, N], U8)
        xt_staged = sbuf("xt_staged", [P, 2, T], U8)
        so_t = sbuf("so_t", [P, FEATURE_TILES], F32)
        sp_t = sbuf("sp_t", [P, FEATURE_TILES], F32)
        bo_t = sbuf("bo_t", [P, FEATURE_TILES], F32)

        def clear(engine, scale_bytes):
            engine.memset(scale_bytes.bitcast(I32), 0)

        clear(nc.gpsimd, ws_folded[:, 0, 0:2 * R])
        clear(nc.gpsimd, ws_folded[:, 0, 2 * R:3 * R])
        clear(nc.vector, xt_staged[0:HALF].rearrange("p h c -> p (h c)"))
        clear(nc.vector, xo_s[:])
        clear(nc.vector, wc_s[:])
        clear(nc.vector, wb_s[:])

        def load_feature_values(queue, tile, values):
            with nc.allow_non_contiguous_dma(reason="one value a partition for each tile of output features"):
                queue.dma_start(tile[:], values.rearrange("(h p) o -> p (h o)", h=FEATURE_TILES))

        flat = "p n t -> p (n t)"
        nc.sync.dma_start(token_list[:], offs)
        load_words(nc.scalar, w_w, w_words[0].rearrange(flat))
        for i, scales in enumerate((w_scales, w2_scales, w0_scales)):
            load_scales_folded((nc.sync, nc.scalar)[i % 2], ws_folded, slice(i * R, (i + 1) * R), scales)
        for quad, queue in enumerate((nc.scalar, nc.sync)):
            load_scales_halved(queue, xt_staged, xt_scales, quad)
        load_words(nc.scalar, xt_w, xt_words[0])
        load_words(nc.sync, w2_w, w2_words[0].rearrange(flat))
        load_words(nc.sync, w0_w, w0_words[0].rearrange(flat))
        for i in range(LIVE):
            load_scale_rows(nc.sync, xo_s, xo_scales, i)
        nc.sync.dma_start(note_list[:], offs2)
        load_words(nc.sync, xo_w, xo_words[0].rearrange(flat))
        nc.sync.dma_start(gate_list[:], offs4)
        load_feature_values(nc.gpsimd, sp_t, sp)
        load_feature_values(nc.gpsimd, bo_t, bo)
        load_words(nc.sync, wb_w, wb_words[0].rearrange(flat))
        load_words(nc.sync, wc_w, wc_words[0])
        for i in range(LIVE):
            load_scale_rows(nc.sync, wc_s, wc_scales, i)
        for i in range(LIVE):
            load_scale_rows(nc.sync, wb_s, wb_scales, i)
        load_feature_values(nc.sync, so_t, so)
        nc.sync.dma_start(value_list[:], offs3)

        xt_gw = sbuf("xt_gw", [P, J], U16)
        xt_gs = sbuf("xt_gs", [P, J], U8)
        xo_gs = sbuf("xo_gs", [P, J], U8)
        w_dw = sbuf("w_dw", [P, R], U32)
        w2_dw = sbuf("w2_dw", [P, R], U32)
        w0_dw = sbuf("w0_dw", [P, R], U32)
        w_ds = sbuf("w_ds", [P, R], U8)
        w2_ds = sbuf("w2_ds", [P, R], U8)
        w0_ds = sbuf("w0_ds", [P, R], U8)

        def deal_words(dealt, words):
            nc.scalar.copy(dealt[:].rearrange("p (t m) -> p m t", t=PACK),
                           words[:].rearrange("p (m t) -> p m t", t=PACK))

        def tile_cols(i):
            return slice(i * P, (i + 1) * P)

        def tile_entries(offsets, jt):
            return offsets[:, jt * P // STRIPE:(jt + 1) * P // STRIPE]

        for quad in range(1, QUADS):
            nc.vector.tensor_copy(ws_folded[QUAD * quad:QUAD * quad + LIVE, 0, :].bitcast(I32),
                                  ws_folded[0:LIVE, quad, :].bitcast(I32))
        for i, dealt in enumerate((w_ds, w2_ds, w0_ds)):
            nc.gpsimd.tensor_copy(dealt[:].rearrange("p (t m) -> p t m", t=PACK),
                                  ws_folded[:, 0, i * R:(i + 1) * R].rearrange("p (m t) -> p t m", t=PACK))
        deal_words(w_dw, w_w)
        for half in range(2):
            nc.vector.tensor_copy(xt_s[half * HALF:(half + 1) * HALF, :].bitcast(I32),
                                  xt_staged[0:HALF, half, :].bitcast(I32))
        for jt in range(SLOT_TILES):
            nc.vector.tensor_copy(xt_gs[:, tile_cols(jt)], xt_s[:].indirect(tile_entries(token_list, jt)))
            nc.vector.tensor_copy(xt_gw[:, tile_cols(jt)], xt_w[:].indirect(tile_entries(token_list, jt)))
        deal_words(w2_dw, w2_w)
        deal_words(w0_dw, w0_w)
        nc.vector.tensor_copy(xo_gs[:], xo_s[:].indirect(note_list[:]))
        xo_gw = sbuf("xo_gw", [P, J], U32, tag="xo_s")
        for jt in range(SLOT_TILES):
            nc.vector.tensor_copy(xo_gw[:, tile_cols(jt)], xo_w[:].indirect(tile_entries(note_list, jt)))

        a_ps = [ps.tile([P, PACK, P], F32, name="a_ps%d" % jt) for jt in range(SLOT_TILES)]
        b_ps = [ps.tile([P, PACK, P], F32, name="b_ps%d" % jt) for jt in range(SLOT_TILES)]
        a_sb = [sbuf("a_sb%d" % jt, [P, P, PACK], F32) for jt in range(SLOT_TILES)]
        for jt in range(SLOT_TILES):
            for t in range(PACK):
                nc.tensor.matmul_mx(a_ps[jt][:, t, :],
                                    lhsT=w_dw[:, tile_cols(t)].bitcast(E5M2), lhsT_scale=w_ds[:, tile_cols(t)],
                                    rhs=xt_gw[:, tile_cols(jt)].bitcast(E2M1), rhs_scale=xt_gs[:, tile_cols(jt)],
                                    start=True, stop=True)
            nc.scalar.copy(a_sb[jt][:], a_ps[jt][:].rearrange("p t j -> p j t"))

        tokens = (w2_dw, w2_ds, xt_gw[:].bitcast(E2M1), xt_gs)
        notes = (w0_dw, w0_ds, xo_gw[:].bitcast(E5M2), xo_gs)
        for term, (weight_w, weight_s, moving_w, moving_s) in enumerate((tokens, notes)):
            for jt in range(SLOT_TILES):
                for t in range(PACK):
                    nc.tensor.matmul_mx(b_ps[jt][:, t, :],
                                        lhsT=weight_w[:, tile_cols(t)].bitcast(E4M3),
                                        lhsT_scale=weight_s[:, tile_cols(t)],
                                        rhs=moving_w[:, tile_cols(jt)], rhs_scale=moving_s[:, tile_cols(jt)],
                                        start=(term == 0 and t == 0), stop=(term == 1 and t == PACK - 1))

        hid = [sbuf("hid%d" % jt, [P, P, PACK], BF16) for jt in range(SLOT_TILES)]
        hid_w = [sbuf("hid_w%d" % jt, [P, P], U32) for jt in range(SLOT_TILES)]
        hid_s = [sbuf("hid_s%d" % jt, [P, P], U8) for jt in range(SLOT_TILES)]
        m0 = [sbuf("m0_%d" % h, [P, J], F32) for h in range(FEATURE_TILES)]
        for jt in range(SLOT_TILES):
            nc.vector.tensor_tensor(hid[jt][:], b_ps[jt][:].rearrange("p t j -> p j t"), a_sb[jt][:], ALU.max)
        for jt in range(SLOT_TILES):
            nc.vector.quantize_mx(hid_w[jt][:].bitcast(E5M2), hid_s[jt][:], hid[jt][:].rearrange("p j t -> p (j t)"))

        for h in range(FEATURE_TILES):
            for jt in range(SLOT_TILES):
                pq = ps.tile([P, 2, P], F32, name="pq%d%d" % (jt, h))
                nc.tensor.matmul_mx(pq[:, 0, :],
                                    lhsT=wb_w[:, tile_cols(h)].bitcast(E4M3), lhsT_scale=wb_s[:, tile_cols(h)],
                                    rhs=hid_w[jt][:].bitcast(E5M2), rhs_scale=hid_s[jt][:], start=True, stop=True)
                nc.tensor.matmul_mx(pq[:, 1, :],
                                    lhsT=wc_w[:, tile_cols(h)].bitcast(E2M1), lhsT_scale=wc_s[:, tile_cols(h)],
                                    rhs=hid_w[jt][:].bitcast(E5M2), rhs_scale=hid_s[jt][:], start=True, stop=True)
                nc.vector.tensor_reduce(m0[h][:, tile_cols(jt)], pq[:].rearrange("p s j -> p j s"), AXIS.X, ALU.max)

        for h in range(FEATURE_TILES):
            gate = sbuf("gate%d" % h, [P, O], F32)
            value = sbuf("value%d" % h, [P, O], F32)
            y = sbuf("y%d" % h, [P, O], F32)
            nc.scalar.activation(gate[:], m0[h][:].indirect(gate_list[:]), ACT.Sigmoid,
                                 bias=bo_t[:, h:h + 1], scale=sp_t[:, h:h + 1])
            nc.scalar.activation(value[:], m0[h][:].indirect(value_list[:]), ACT.Copy, scale=so_t[:, h:h + 1])
            nc.vector.tensor_tensor(y[:], value[:], gate[:], ALU.mult)
            nc.sync.dma_start(out[tile_cols(h), :], y[:])
